import numpy as np
import ml_dtypes


def mxq(x, axis, fmt="e4m3"):
    dtype, down = {"e4m3": (ml_dtypes.float8_e4m3fn, 7), "e5m2": (ml_dtypes.float8_e5m2, 14)}[fmt]
    v = np.moveaxis(np.asarray(x, np.float32).astype(ml_dtypes.bfloat16).astype(np.float64), axis, -1)
    blocks = v.reshape(v.shape[:-1] + (-1, 32))
    amax = np.abs(blocks).max(-1, keepdims=True)
    byte = np.maximum(np.where(amax > 0, np.frexp(amax)[1] - 1 + 127, 0) - down, 1)
    scale = np.exp2(byte - 127.0)
    codes = (blocks / scale).astype(np.float32).astype(dtype).astype(np.float64)
    return np.moveaxis((codes * scale).reshape(v.shape), -1, axis)


WIDE = False


def mx_kscale(k):
    if not WIDE:
        return np.ones(k)
    levels = np.array([10, -10, 5, -5, 0])
    if k % 512:
        return np.exp2(np.random.permutation(np.resize(levels, k // 32))).repeat(32)
    a = np.empty((k // 512, 16))
    for p in range(k // 512):
        a[p, :8] = np.random.permutation(np.resize(levels, 8))
        for g in range(8):
            far = levels[np.abs(levels - a[p, g]) >= 10]
            a[p, g + 8] = far[np.random.randint(len(far))]
    return np.exp2(a.ravel()).repeat(32)


def f64(x):
    return np.asarray(x).astype(np.float64)


def striped(idx):
    return np.tile(idx.reshape(-1, 16).T, (8, 1)).astype(np.uint16)


def unstriped(offs):
    return offs[:16].T.reshape(-1).astype(np.int64)


def pack_weight(w):
    k, n = w.shape
    w = f64(np.asarray(w, np.float32).astype(ml_dtypes.bfloat16)).reshape(k // 32, 32, n)
    amax = np.abs(w).max(1)
    byte = np.clip(np.where(amax > 0, np.frexp(amax)[1] - 1 + 127 - 7, 1), 1, 254)
    scaled = (w * np.exp2(127.0 - byte)[:, None, :]).reshape(k, n).astype(np.float32)
    words = np.ascontiguousarray(scaled.reshape(k // 512, 128, 4, n).transpose(0, 1, 3, 2)).astype(ml_dtypes.float8_e4m3fn).view(np.uint8)
    return words, np.ascontiguousarray(byte.astype(np.uint8).reshape(k // 512, 16, n))


def unpack_weight(words, scales):
    g, p, n, _ = words.shape
    vals = np.ascontiguousarray(words).view(ml_dtypes.float8_e4m3fn).astype(np.float64) * np.repeat(np.exp2(scales.astype(np.float64) - 127.0), 8, axis=1)[..., None]
    return vals.transpose(0, 1, 3, 2).reshape(g * 512, n)


def relu(v):
    return np.maximum(v, 0.0)


K, T, S, D, N, V = 1024, 4096, 1024, 4, 128, 256


def setup_inputs():
    n = np.random.standard_normal
    s = mx_kscale(K)[:, None]
    packed_xT = pack_weight(n((K, T)) * s)
    return {
        "x_words": packed_xT[0],
        "x_scales": packed_xT[1],
        "w1": (n((K, N)) / np.sqrt(K) / s).astype(np.float32),
        "rest": (-np.random.uniform(0.5, 4.0, (N, 1))).astype(np.float32),
        "offs": striped(np.random.permutation(T)[:S]),
        "nbr": striped(np.random.permutation(np.concatenate([np.arange(V), np.random.randint(0, V, S - V)]))),
    }


def reference(x_words, x_scales, w1, rest, offs, nbr):
    xq = unpack_weight(x_words, x_scales)[:, unstriped(offs)]
    y = mxq(f64(w1), 0, "e4m3").T @ xq
    rr = 0.5 * ((y) ** 2)
    ker = (relu(-0.4 * rr + 1.0)) ** 2
    dens = ker.reshape(len(ker), -1, D).sum(axis=2) + 0.6
    pres = (dens) ** 2 + f64(rest)
    pd = pres / ((dens) ** 2)
    return ((np.repeat(pd, D, axis=1) + pd[:, unstriped(nbr)]) * relu(-0.4 * rr + 1.0)) * y

@@ -1,0 +1,192 @@
+from contextlib import ExitStack
+
+import concourse.mybir as mybir
+
+K, T, S, D, N, V = 1024, 4096, 1024, 4, 128, 256
+FLOPS = 2 * K * N * S
+
+F32 = mybir.dt.float32
+BF16 = mybir.dt.bfloat16
+I32 = mybir.dt.int32
+U32 = mybir.dt.uint32
+U16 = mybir.dt.uint16
+U8 = mybir.dt.uint8
+FP8X4 = mybir.dt.float8_e4m3fn_x4
+ACT = mybir.ActivationFunctionType
+ALU = mybir.AluOpType
+AX = mybir.AxisListType
+
+P = 128
+PACK = 4
+PASSES = K // (P * PACK)
+LIST_ROWS = 16
+HALF = S // 2
+CHUNK = 256
+CHUNKS = S // CHUNK
+FAR = [224,224,224,224,128]
+U_ON_SCALAR = [1,1,0,0]
+
+
+def tile_picked_ysph_force_p_kernel(tc, x_words, x_scales, w1, rest, offs, nbr, out):
+    nc = tc.nc
+    with ExitStack() as ctx:
+        keep = ctx.enter_context(tc.tile_pool(name="keep", bufs=1))
+        psum = ctx.enter_context(tc.psum_pool(name="psum", bufs=1))
+
+        offs_sb = keep.tile([P, S // LIST_ROWS], U16, name="offs_sb")
+        nbr_sb = keep.tile([P, S // LIST_ROWS], U16, name="nbr_sb")
+        rest_sb = keep.tile([P, 1], F32, name="rest_sb")
+        words = [keep.tile([P, T], U32, name="words%d" % o, align_bytes=64) for o in range(PASSES)]
+        scales = keep.tile([P, T], U8, name="scales", tag="scales", align_bytes=64)
+
+        one = keep.tile([P, 1], F32, name="one")
+        warm = keep.tile([P, 1], F32, name="warm")
+        nc.vector.memset(scales[:].bitcast(I32), 0)
+        nc.vector.memset(one[:], 1.0)
+        nc.scalar.activation(out=warm[:], in_=one[:], func=ACT.Abs_reciprocal_sqrt)
+
+        def load_words(o):
+            nc.sync.dma_start(out=words[o][:].bitcast(I32), in_=x_words[o].rearrange("p c r -> p (c r)").bitcast(I32))
+
+        w_codes = [keep.tile([P, N], U32, name="w_codes%d" % o, align_bytes=64) for o in range(PASSES)]
+        w_scales = [keep.tile([P, N], U8, name="w_scales%d" % o, align_bytes=64) for o in range(PASSES)]
+
+        def round_w(o):
+            raw = keep.tile([P, PACK, N], F32, name="w_raw")
+            rows = w1[o * P * PACK : (o + 1) * P * PACK, :]
+            nc.sync.dma_start(out=raw[:], in_=rows.rearrange("(p j) m -> p j m", j=PACK))
+            grouped = keep.tile([P, N, PACK], BF16, name="grouped%d" % o, align_bytes=64)
+            nc.scalar.copy(out=grouped[:], in_=raw[:].rearrange("p j m -> p m j"))
+            return grouped
+
+        def quantise_w(o, grouped):
+            nc.vector.quantize_mx(
+                out=w_codes[o][:].bitcast(FP8X4),
+                scales=w_scales[o][:],
+                in_=grouped[:].rearrange("p m j -> p (m j)"),
+            )
+
+        nc.sync.dma_start(offs_sb[:], offs)
+        load_words(0)
+        for q in range(4):
+            nc.gpsimd.dma_start(
+                out=scales[32 * q : 32 * q + 4 * PASSES, :].bitcast(I32),
+                in_=x_scales[:, 4 * q : 4 * q + 4, :].bitcast(I32),
+            )
+        grouped0 = round_w(0)
+        load_words(1)
+        grouped1 = round_w(1)
+        nc.sync.dma_start(nbr_sb[:], nbr)
+        nc.sync.dma_start(out=rest_sb[:], in_=rest)
+
+        picked_scales = keep.tile([P, S], U8, name="picked_scales", align_bytes=64)
+        y = [psum.tile([N, CHUNK], F32, name="y%d" % c) for c in range(CHUNKS)]
+
+        def pick_words(o, h):
+            name = "picked%d_%d" % (o, h)
+            tag = "scales" if (o, h) == (1, 0) else name
+            picked = keep.tile([P, HALF], U32, name=name, tag=tag, align_bytes=64)
+            cols = slice(h * HALF // LIST_ROWS, (h + 1) * HALF // LIST_ROWS)
+            nc.vector.tensor_copy(picked[:], words[o][:].indirect(offs_sb[:, cols]))
+            return picked
+
+        def multiply(o, h, picked):
+            for first in range(0, HALF, CHUNK):
+                c = (h * HALF + first) // CHUNK
+                nc.tensor.matmul_mx(
+                    out=y[c][:],
+                    lhsT=w_codes[o][:].bitcast(FP8X4),
+                    lhsT_scale=w_scales[o][:],
+                    rhs=picked[:, first : first + CHUNK].bitcast(FP8X4),
+                    rhs_scale=picked_scales[4 * o : P, c * CHUNK : (c + 1) * CHUNK],
+                    start=(o == 0),
+                    stop=(o == PASSES - 1),
+                )
+
+        nc.vector.tensor_copy(picked_scales[:], scales[:].indirect(offs_sb[:]))
+        first_half = pick_words(0, 0)
+        quantise_w(0, grouped0)
+        multiply(0, 0, first_half)
+        multiply(0, 1, pick_words(0, 1))
+        first_half = pick_words(1, 0)
+        quantise_w(1, grouped1)
+        multiply(1, 0, first_half)
+        multiply(1, 1, pick_words(1, 1))
+
+        ysq = [keep.tile([N, CHUNK], F32, name="ysq%d" % c) for c in range(CHUNKS)]
+        u = [keep.tile([N, CHUNK], F32, name="u%d" % c) for c in range(CHUNKS)]
+        ker = [keep.tile([N, CHUNK], F32, name="ker%d" % c) for c in range(CHUNKS)]
+        uy = keep.tile([N, S], F32, name="uy")
+        ksum = keep.tile([N, V], F32, name="ksum")
+        dsq = keep.tile([N, V], F32, name="dsq")
+        inv = keep.tile([N, V], F32, name="inv")
+        q_all = keep.tile([N, V], F32, name="q_all")
+
+        def kernel_values(c):
+            nc.scalar.activation(out=ysq[c][:], in_=y[c][:], func=ACT.Square)
+            if U_ON_SCALAR[c]:
+                nc.scalar.activation(out=u[c][:], in_=ysq[c][:], func=ACT.Relu, scale=-0.2, bias=1.0)
+                nc.scalar.activation(out=ker[c][:], in_=u[c][:], func=ACT.Square)
+            else:
+                nc.vector.tensor_scalar(
+                    out=u[c][:], in0=ysq[c][:], scalar1=5.0, scalar2=5.0, op0=ALU.min, op1=ALU.subtract
+                )
+                nc.scalar.activation(out=ker[c][:], in_=u[c][:], func=ACT.Square, scale=0.2)
+
+        def density(c):
+            groups = slice(c * CHUNK // D, (c + 1) * CHUNK // D)
+            nc.vector.tensor_reduce(
+                out=ksum[:, groups], in_=ker[c][:].rearrange("m (v d) -> m v d", d=D), axis=AX.X, op=ALU.add
+            )
+
+        def pressure(first, last):
+            pair = slice(first * CHUNK // D, last * CHUNK // D)
+            nc.scalar.activation(out=dsq[:, pair], in_=ksum[:, pair], func=ACT.Square, bias=0.6)
+            nc.scalar.activation(out=inv[:, pair], in_=dsq[:, pair], func=ACT.Abs_reciprocal_sqrt)
+            nc.vector.scalar_tensor_tensor(
+                out=q_all[:, pair], in0=inv[:, pair], scalar=rest_sb[:], in1=inv[:, pair], op0=ALU.mult, op1=ALU.mult
+            )
+
+        def slope(c):
+            cols = slice(c * CHUNK, (c + 1) * CHUNK)
+            if U_ON_SCALAR[c]:
+                nc.vector.tensor_tensor(out=uy[:, cols], in0=y[c][:], in1=u[c][:], op=ALU.mult)
+            else:
+                nc.vector.scalar_tensor_tensor(
+                    out=uy[:, cols], in0=y[c][:], scalar=-0.2, in1=u[c][:], op0=ALU.mult, op1=ALU.mult
+                )
+
+        for c in range(CHUNKS):
+            kernel_values(c)
+        density(0)
+        density(1)
+        pressure(0, 2)
+        density(2)
+        density(3)
+        pressure(2, 4)
+        for c in range(CHUNKS):
+            slope(c)
+
+        first = 0
+        for i, width in enumerate(FAR):
+            last = first + width
+            cols = slice(first, last)
+            count = width // D
+            own = keep.tile([N, width], F32, name="own%d" % i)
+            both = keep.tile([N, width], F32, name="both%d" % i)
+            force = keep.tile([N, width], F32, name="force%d" % i)
+            nc.scalar.activation(
+                out=own[:].rearrange("m (v d) -> m v d", d=D),
+                in_=q_all[:, first // D : last // D].unsqueeze(2).to_broadcast([N, count, D]),
+                func=ACT.Identity,
+                bias=2.0,
+            )
+            nc.vector.tensor_tensor(
+                both[:],
+                q_all[:].indirect(nbr_sb[:, first // LIST_ROWS : last // LIST_ROWS]),
+                own[:],
+                ALU.add,
+            )
+            nc.vector.tensor_tensor(out=force[:], in0=both[:], in1=uy[:, cols], op=ALU.mult)
+            nc.sync.dma_start(out=out[:, cols], in_=force[:])
+            first = last

@@ -21,10 +21,13 @@ PACK = 4
 PASSES = K // (P * PACK)
 LIST_ROWS = 16
 HALF = S // 2
-CHUNK = 256
-CHUNKS = S // CHUNK
+CHUNKS = [256,256,256,256]
+STARTS = [sum(CHUNKS[:c]) for c in range(len(CHUNKS) + 1)]
 FAR = [224,224,224,224,128]
-U_ON_SCALAR = [1,1,0,0]
+CLAMP_ENGINE = "SSVV"
+KER_ENGINE = "SSSS"
+ORDER = "s0 m0 s1 k0 m1 k1 s2 s3 r0 m2 m3 r1 k2 k3 r2 r3 p0 p1 y0 y1 y2 y3".split()
+PRESSURE_CUTS = [0,3,4]
 
 
 def tile_picked_ysph_force_p_kernel(tc, x_words, x_scales, w1, rest, offs, nbr, out):
@@ -36,136 +39,139 @@ def tile_picked_ysph_force_p_kernel(tc, x_words, x_scales, w1, rest, offs, nbr, 
         offs_sb = keep.tile([P, S // LIST_ROWS], U16, name="offs_sb")
         nbr_sb = keep.tile([P, S // LIST_ROWS], U16, name="nbr_sb")
         rest_sb = keep.tile([P, 1], F32, name="rest_sb")
-        words = [keep.tile([P, T], U32, name="words%d" % o, align_bytes=64) for o in range(PASSES)]
+        rest_scaled = keep.tile([P, 1], F32, name="rest_scaled")
         scales = keep.tile([P, T], U8, name="scales", tag="scales", align_bytes=64)
 
         one = keep.tile([P, 1], F32, name="one")
-        warm = keep.tile([P, 1], F32, name="warm")
+        warm = keep.tile([P, 1], F32, name="warm", tag="warm", align_bytes=64)
         nc.vector.memset(scales[:].bitcast(I32), 0)
         nc.vector.memset(one[:], 1.0)
         nc.scalar.activation(out=warm[:], in_=one[:], func=ACT.Abs_reciprocal_sqrt)
 
+        words = [keep.tile([P, T], U32, name="words%d" % o, tag="words%d" % o, align_bytes=64) for o in range(PASSES)]
+
         def load_words(o):
             nc.sync.dma_start(out=words[o][:].bitcast(I32), in_=x_words[o].rearrange("p c r -> p (c r)").bitcast(I32))
 
-        w_codes = [keep.tile([P, N], U32, name="w_codes%d" % o, align_bytes=64) for o in range(PASSES)]
-        w_scales = [keep.tile([P, N], U8, name="w_scales%d" % o, align_bytes=64) for o in range(PASSES)]
-
-        def round_w(o):
-            raw = keep.tile([P, PACK, N], F32, name="w_raw")
-            rows = w1[o * P * PACK : (o + 1) * P * PACK, :]
-            nc.sync.dma_start(out=raw[:], in_=rows.rearrange("(p j) m -> p j m", j=PACK))
-            grouped = keep.tile([P, N, PACK], BF16, name="grouped%d" % o, align_bytes=64)
-            nc.scalar.copy(out=grouped[:], in_=raw[:].rearrange("p j m -> p m j"))
-            return grouped
-
-        def quantise_w(o, grouped):
-            nc.vector.quantize_mx(
-                out=w_codes[o][:].bitcast(FP8X4),
-                scales=w_scales[o][:],
-                in_=grouped[:].rearrange("p m j -> p (m j)"),
-            )
+        w_raw = keep.tile([P, PASSES, PACK, N], F32, name="w_raw")
+        grouped = keep.tile([P, PASSES, N, PACK], BF16, name="grouped", align_bytes=64)
+        w_codes = keep.tile([P, PASSES, N], U32, name="w_codes", align_bytes=64)
+        w_scales = keep.tile([P, PASSES, N], U8, name="w_scales", align_bytes=64)
 
         nc.sync.dma_start(offs_sb[:], offs)
         load_words(0)
+        nc.sync.dma_start(out=w_raw[:], in_=w1.rearrange("(o p j) m -> p o j m", o=PASSES, j=PACK))
+        nc.sync.dma_start(nbr_sb[:], nbr)
         for q in range(4):
             nc.gpsimd.dma_start(
                 out=scales[32 * q : 32 * q + 4 * PASSES, :].bitcast(I32),
                 in_=x_scales[:, 4 * q : 4 * q + 4, :].bitcast(I32),
             )
-        grouped0 = round_w(0)
         load_words(1)
-        grouped1 = round_w(1)
-        nc.sync.dma_start(nbr_sb[:], nbr)
         nc.sync.dma_start(out=rest_sb[:], in_=rest)
+        nc.scalar.activation(out=rest_scaled[:], in_=rest_sb[:], func=ACT.Copy, scale=-0.2)
 
         picked_scales = keep.tile([P, S], U8, name="picked_scales", align_bytes=64)
-        y = [psum.tile([N, CHUNK], F32, name="y%d" % c) for c in range(CHUNKS)]
+        y = [psum.tile([N, width], F32, name="y%d" % c) for c, width in enumerate(CHUNKS)]
 
-        def pick_words(o, h):
-            name = "picked%d_%d" % (o, h)
-            tag = "scales" if (o, h) == (1, 0) else name
-            picked = keep.tile([P, HALF], U32, name=name, tag=tag, align_bytes=64)
-            cols = slice(h * HALF // LIST_ROWS, (h + 1) * HALF // LIST_ROWS)
-            nc.vector.tensor_copy(picked[:], words[o][:].indirect(offs_sb[:, cols]))
+        def pick_words(o):
+            picked = []
+            for h in range(2):
+                tag = (("picked_a", "picked_b"), ("scales", "picked_a"))[o][h]
+                half = keep.tile([P, HALF], U32, name="picked%d_%d" % (o, h), tag=tag, align_bytes=64)
+                cols = slice(h * HALF // LIST_ROWS, (h + 1) * HALF // LIST_ROWS)
+                nc.vector.tensor_copy(half[:], words[o][:].indirect(offs_sb[:, cols]))
+                picked.append(half)
             return picked
 
-        def multiply(o, h, picked):
-            for first in range(0, HALF, CHUNK):
-                c = (h * HALF + first) // CHUNK
+        def multiply(o, picked):
+            for c in range(len(CHUNKS)):
+                cols = slice(STARTS[c], STARTS[c + 1])
                 nc.tensor.matmul_mx(
                     out=y[c][:],
-                    lhsT=w_codes[o][:].bitcast(FP8X4),
-                    lhsT_scale=w_scales[o][:],
-                    rhs=picked[:, first : first + CHUNK].bitcast(FP8X4),
-                    rhs_scale=picked_scales[4 * o : P, c * CHUNK : (c + 1) * CHUNK],
+                    lhsT=w_codes[:, o, :].bitcast(FP8X4),
+                    lhsT_scale=w_scales[:, o, :],
+                    rhs=picked[STARTS[c] // HALF][:, STARTS[c] % HALF : STARTS[c] % HALF + CHUNKS[c]].bitcast(FP8X4),
+                    rhs_scale=picked_scales[4 * o : P, cols],
                     start=(o == 0),
                     stop=(o == PASSES - 1),
                 )
 
+        nc.scalar.copy(out=grouped[:], in_=w_raw[:].rearrange("p o j m -> p o m j"))
         nc.vector.tensor_copy(picked_scales[:], scales[:].indirect(offs_sb[:]))
-        first_half = pick_words(0, 0)
-        quantise_w(0, grouped0)
-        multiply(0, 0, first_half)
-        multiply(0, 1, pick_words(0, 1))
-        first_half = pick_words(1, 0)
-        quantise_w(1, grouped1)
-        multiply(1, 0, first_half)
-        multiply(1, 1, pick_words(1, 1))
+        picked0 = pick_words(0)
+        nc.vector.quantize_mx(
+            out=w_codes[:].rearrange("p o m -> p (o m)").bitcast(FP8X4),
+            scales=w_scales[:].rearrange("p o m -> p (o m)"),
+            in_=grouped[:].rearrange("p o m j -> p (o m j)"),
+        )
+        multiply(0, picked0)
+        multiply(1, pick_words(1))
 
-        ysq = [keep.tile([N, CHUNK], F32, name="ysq%d" % c) for c in range(CHUNKS)]
-        u = [keep.tile([N, CHUNK], F32, name="u%d" % c) for c in range(CHUNKS)]
-        ker = [keep.tile([N, CHUNK], F32, name="ker%d" % c) for c in range(CHUNKS)]
+        ysq = [keep.tile([N, width], F32, name="ysq%d" % c) for c, width in enumerate(CHUNKS)]
+        u = [keep.tile([N, width], F32, name="u%d" % c) for c, width in enumerate(CHUNKS)]
+        ker = [keep.tile([N, width], F32, name="ker%d" % c) for c, width in enumerate(CHUNKS)]
         uy = keep.tile([N, S], F32, name="uy")
         ksum = keep.tile([N, V], F32, name="ksum")
         dsq = keep.tile([N, V], F32, name="dsq")
         inv = keep.tile([N, V], F32, name="inv")
         q_all = keep.tile([N, V], F32, name="q_all")
 
-        def kernel_values(c):
+        def square(c):
             nc.scalar.activation(out=ysq[c][:], in_=y[c][:], func=ACT.Square)
-            if U_ON_SCALAR[c]:
-                nc.scalar.activation(out=u[c][:], in_=ysq[c][:], func=ACT.Relu, scale=-0.2, bias=1.0)
-                nc.scalar.activation(out=ker[c][:], in_=u[c][:], func=ACT.Square)
-            else:
+
+        def clamp(c):
+            if CLAMP_ENGINE[c] == "S":
+                nc.scalar.activation(out=u[c][:], in_=ysq[c][:], func=ACT.Relu, scale=-1.0, bias=5.0)
+            elif CLAMP_ENGINE[c] == "V":
                 nc.vector.tensor_scalar(
                     out=u[c][:], in0=ysq[c][:], scalar1=5.0, scalar2=5.0, op0=ALU.min, op1=ALU.subtract
                 )
+            else:
+                nc.gpsimd.tensor_scalar(
+                    out=u[c][:], in0=ysq[c][:], scalar1=5.0, scalar2=0.0, op0=ALU.min, op1=ALU.max
+                )
+
+        def kernel_value(c):
+            if KER_ENGINE[c] == "V":
+                nc.vector.scalar_tensor_tensor(
+                    out=ker[c][:], in0=u[c][:], scalar=0.04, in1=u[c][:], op0=ALU.mult, op1=ALU.mult
+                )
+            elif CLAMP_ENGINE[c] == "G":
+                nc.scalar.activation(out=ker[c][:], in_=u[c][:], func=ACT.Square, scale=-0.2, bias=1.0)
+            else:
                 nc.scalar.activation(out=ker[c][:], in_=u[c][:], func=ACT.Square, scale=0.2)
 
         def density(c):
-            groups = slice(c * CHUNK // D, (c + 1) * CHUNK // D)
+            groups = slice(STARTS[c] // D, STARTS[c + 1] // D)
             nc.vector.tensor_reduce(
                 out=ksum[:, groups], in_=ker[c][:].rearrange("m (v d) -> m v d", d=D), axis=AX.X, op=ALU.add
             )
 
-        def pressure(first, last):
-            pair = slice(first * CHUNK // D, last * CHUNK // D)
-            nc.scalar.activation(out=dsq[:, pair], in_=ksum[:, pair], func=ACT.Square, bias=0.6)
-            nc.scalar.activation(out=inv[:, pair], in_=dsq[:, pair], func=ACT.Abs_reciprocal_sqrt)
+        def pressure(g):
+            first, last = PRESSURE_CUTS[g], PRESSURE_CUTS[g + 1]
+            groups = slice(STARTS[first] // D, STARTS[last] // D)
+            nc.scalar.activation(out=dsq[:, groups], in_=ksum[:, groups], func=ACT.Square, bias=0.6)
+            nc.scalar.activation(out=inv[:, groups], in_=dsq[:, groups], func=ACT.Abs_reciprocal_sqrt)
             nc.vector.scalar_tensor_tensor(
-                out=q_all[:, pair], in0=inv[:, pair], scalar=rest_sb[:], in1=inv[:, pair], op0=ALU.mult, op1=ALU.mult
+                out=q_all[:, groups],
+                in0=inv[:, groups],
+                scalar=rest_scaled[:],
+                in1=inv[:, groups],
+                op0=ALU.mult,
+                op1=ALU.mult,
             )
 
         def slope(c):
-            cols = slice(c * CHUNK, (c + 1) * CHUNK)
-            if U_ON_SCALAR[c]:
-                nc.vector.tensor_tensor(out=uy[:, cols], in0=y[c][:], in1=u[c][:], op=ALU.mult)
-            else:
-                nc.vector.scalar_tensor_tensor(
-                    out=uy[:, cols], in0=y[c][:], scalar=-0.2, in1=u[c][:], op0=ALU.mult, op1=ALU.mult
-                )
+            cols = slice(STARTS[c], STARTS[c + 1])
+            scalar, op0 = {"S": (-1.0, ALU.mult), "V": (1.0, ALU.mult), "G": (5.0, ALU.subtract)}[CLAMP_ENGINE[c]]
+            nc.vector.scalar_tensor_tensor(
+                out=uy[:, cols], in0=u[c][:], scalar=scalar, in1=y[c][:], op0=op0, op1=ALU.mult
+            )
 
-        for c in range(CHUNKS):
-            kernel_values(c)
-        density(0)
-        density(1)
-        pressure(0, 2)
-        density(2)
-        density(3)
-        pressure(2, 4)
-        for c in range(CHUNKS):
-            slope(c)
+        steps = {"s": square, "m": clamp, "k": kernel_value, "r": density, "p": pressure, "y": slope}
+        for step in ORDER:
+            steps[step[0]](int(step[1]))
 
         first = 0
         for i, width in enumerate(FAR):
@@ -179,7 +185,7 @@ def tile_picked_ysph_force_p_kernel(tc, x_words, x_scales, w1, rest, offs, nbr, 
                 out=own[:].rearrange("m (v d) -> m v d", d=D),
                 in_=q_all[:, first // D : last // D].unsqueeze(2).to_broadcast([N, count, D]),
                 func=ACT.Identity,
-                bias=2.0,
+                bias=-0.4,
             )
             nc.vector.tensor_tensor(
                 both[:],

@@ -21,13 +21,13 @@ PACK = 4
 PASSES = K // (P * PACK)
 LIST_ROWS = 16
 HALF = S // 2
-CHUNKS = [256,256,256,256]
+CHUNKS = [256,256,256,128,128]
 STARTS = [sum(CHUNKS[:c]) for c in range(len(CHUNKS) + 1)]
-FAR = [224,224,224,224,128]
-CLAMP_ENGINE = "SSVV"
-KER_ENGINE = "SSSS"
-ORDER = "s0 m0 s1 k0 m1 k1 s2 s3 r0 m2 m3 r1 k2 k3 r2 r3 p0 p1 y0 y1 y2 y3".split()
-PRESSURE_CUTS = [0,3,4]
+FAR = [256,384,256,128]
+CLAMP_ENGINE = "VVVVV"
+KER_ENGINE = "SVSSS"
+ORDER = "s0 s1 m0 m1 k0 k1 s2 s3 s4 r0 m2 r1 m3 m4 k2 k3 k4 r2 r3 r4 p0 p1 y0 y1 y2 y3 y4".split()
+PRESSURE_CUTS = [0,3,5]
 
 
 def tile_picked_ysph_force_p_kernel(tc, x_words, x_scales, w1, rest, offs, nbr, out):
@@ -48,27 +48,35 @@ def tile_picked_ysph_force_p_kernel(tc, x_words, x_scales, w1, rest, offs, nbr, 
         nc.vector.memset(one[:], 1.0)
         nc.scalar.activation(out=warm[:], in_=one[:], func=ACT.Abs_reciprocal_sqrt)
 
-        words = [keep.tile([P, T], U32, name="words%d" % o, tag="words%d" % o, align_bytes=64) for o in range(PASSES)]
+        words = {}
 
         def load_words(o):
+            words[o] = keep.tile([P, T], U32, name="words%d" % o, tag=("words0", "w_raw")[o], align_bytes=64)
             nc.sync.dma_start(out=words[o][:].bitcast(I32), in_=x_words[o].rearrange("p c r -> p (c r)").bitcast(I32))
 
-        w_raw = keep.tile([P, PASSES, PACK, N], F32, name="w_raw")
+        w_raw = keep.tile([P, PASSES, PACK, N], F32, name="w_raw", tag="w_raw", align_bytes=64)
         grouped = keep.tile([P, PASSES, N, PACK], BF16, name="grouped", align_bytes=64)
         w_codes = keep.tile([P, PASSES, N], U32, name="w_codes", align_bytes=64)
         w_scales = keep.tile([P, PASSES, N], U8, name="w_scales", align_bytes=64)
 
         nc.sync.dma_start(offs_sb[:], offs)
-        load_words(0)
         nc.sync.dma_start(out=w_raw[:], in_=w1.rearrange("(o p j) m -> p o j m", o=PASSES, j=PACK))
+        load_words(0)
         nc.sync.dma_start(nbr_sb[:], nbr)
-        for q in range(4):
+        nc.sync.dma_start(out=rest_sb[:], in_=rest)
+        for q in range(2):
             nc.gpsimd.dma_start(
                 out=scales[32 * q : 32 * q + 4 * PASSES, :].bitcast(I32),
                 in_=x_scales[:, 4 * q : 4 * q + 4, :].bitcast(I32),
             )
+        for q in range(2, 4):
+            for o in range(PASSES):
+                nc.sync.dma_start(
+                    out=scales[32 * q + 4 * o : 32 * q + 4 * o + 4, :].bitcast(I32),
+                    in_=x_scales[o, 4 * q : 4 * q + 4, :].bitcast(I32),
+                )
+        nc.scalar.copy(out=grouped[:], in_=w_raw[:].rearrange("p o j m -> p o m j"))
         load_words(1)
-        nc.sync.dma_start(out=rest_sb[:], in_=rest)
         nc.scalar.activation(out=rest_scaled[:], in_=rest_sb[:], func=ACT.Copy, scale=-0.2)
 
         picked_scales = keep.tile([P, S], U8, name="picked_scales", align_bytes=64)
@@ -97,7 +105,6 @@ def tile_picked_ysph_force_p_kernel(tc, x_words, x_scales, w1, rest, offs, nbr, 
                     stop=(o == PASSES - 1),
                 )
 
-        nc.scalar.copy(out=grouped[:], in_=w_raw[:].rearrange("p o j m -> p o m j"))
         nc.vector.tensor_copy(picked_scales[:], scales[:].indirect(offs_sb[:]))
         picked0 = pick_words(0)
         nc.vector.quantize_mx(
@@ -110,12 +117,11 @@ def tile_picked_ysph_force_p_kernel(tc, x_words, x_scales, w1, rest, offs, nbr, 
 
         ysq = [keep.tile([N, width], F32, name="ysq%d" % c) for c, width in enumerate(CHUNKS)]
         u = [keep.tile([N, width], F32, name="u%d" % c) for c, width in enumerate(CHUNKS)]
-        ker = [keep.tile([N, width], F32, name="ker%d" % c) for c, width in enumerate(CHUNKS)]
         uy = keep.tile([N, S], F32, name="uy")
+        ker = [uy[:, STARTS[c] : STARTS[c + 1]] for c in range(len(CHUNKS))]
         ksum = keep.tile([N, V], F32, name="ksum")
-        dsq = keep.tile([N, V], F32, name="dsq")
-        inv = keep.tile([N, V], F32, name="inv")
-        q_all = keep.tile([N, V], F32, name="q_all")
+        table = keep.tile([N, 3 * V], F32, name="table")
+        q_all, inv, dsq = table[:, 0:V], table[:, V : 2 * V], table[:, 2 * V : 3 * V]
 
         def square(c):
             nc.scalar.activation(out=ysq[c][:], in_=y[c][:], func=ACT.Square)
@@ -135,17 +141,17 @@ def tile_picked_ysph_force_p_kernel(tc, x_words, x_scales, w1, rest, offs, nbr, 
         def kernel_value(c):
             if KER_ENGINE[c] == "V":
                 nc.vector.scalar_tensor_tensor(
-                    out=ker[c][:], in0=u[c][:], scalar=0.04, in1=u[c][:], op0=ALU.mult, op1=ALU.mult
+                    out=ker[c], in0=u[c][:], scalar=0.04, in1=u[c][:], op0=ALU.mult, op1=ALU.mult
                 )
             elif CLAMP_ENGINE[c] == "G":
-                nc.scalar.activation(out=ker[c][:], in_=u[c][:], func=ACT.Square, scale=-0.2, bias=1.0)
+                nc.scalar.activation(out=ker[c], in_=u[c][:], func=ACT.Square, scale=-0.2, bias=1.0)
             else:
-                nc.scalar.activation(out=ker[c][:], in_=u[c][:], func=ACT.Square, scale=0.2)
+                nc.scalar.activation(out=ker[c], in_=u[c][:], func=ACT.Square, scale=0.2)
 
         def density(c):
             groups = slice(STARTS[c] // D, STARTS[c + 1] // D)
             nc.vector.tensor_reduce(
-                out=ksum[:, groups], in_=ker[c][:].rearrange("m (v d) -> m v d", d=D), axis=AX.X, op=ALU.add
+                out=ksum[:, groups], in_=ker[c].rearrange("m (v d) -> m v d", d=D), axis=AX.X, op=ALU.add
             )
 
         def pressure(g):
@@ -189,7 +195,7 @@ def tile_picked_ysph_force_p_kernel(tc, x_words, x_scales, w1, rest, offs, nbr, 
             )
             nc.vector.tensor_tensor(
                 both[:],
-                q_all[:].indirect(nbr_sb[:, first // LIST_ROWS : last // LIST_ROWS]),
+                table[:].indirect(nbr_sb[:, first // LIST_ROWS : last // LIST_ROWS]),
                 own[:],
                 ALU.add,
             )

from contextlib import ExitStack

import concourse.mybir as mybir

K, T, S, D, N, V = 1024, 4096, 1024, 4, 128, 256
FLOPS = 2 * K * N * S

F32 = mybir.dt.float32
BF16 = mybir.dt.bfloat16
I32 = mybir.dt.int32
U32 = mybir.dt.uint32
U16 = mybir.dt.uint16
U8 = mybir.dt.uint8
FP8X4 = mybir.dt.float8_e4m3fn_x4
ACT = mybir.ActivationFunctionType
ALU = mybir.AluOpType
AX = mybir.AxisListType

P = 128
PACK = 4
PASSES = K // (P * PACK)
LIST_ROWS = 16
HALF = S // 2
CHUNKS = [256,256,256,128,128]
STARTS = [sum(CHUNKS[:c]) for c in range(len(CHUNKS) + 1)]
FAR = [256,384,256,128]
CLAMP_ENGINE = "VVVVV"
KER_ENGINE = "SVSSS"
ORDER = "s0 s1 m0 m1 k0 k1 s2 s3 s4 r0 m2 r1 m3 m4 k2 k3 k4 r2 r3 r4 p0 p1 y0 y1 y2 y3 y4".split()
PRESSURE_CUTS = [0,3,5]


def tile_picked_ysph_force_p_kernel(tc, x_words, x_scales, w1, rest, offs, nbr, out):
    nc = tc.nc
    with ExitStack() as ctx:
        keep = ctx.enter_context(tc.tile_pool(name="keep", bufs=1))
        psum = ctx.enter_context(tc.psum_pool(name="psum", bufs=1))

        offs_sb = keep.tile([P, S // LIST_ROWS], U16, name="offs_sb")
        nbr_sb = keep.tile([P, S // LIST_ROWS], U16, name="nbr_sb")
        rest_sb = keep.tile([P, 1], F32, name="rest_sb")
        rest_scaled = keep.tile([P, 1], F32, name="rest_scaled")
        scales = keep.tile([P, T], U8, name="scales", tag="scales", align_bytes=64)

        one = keep.tile([P, 1], F32, name="one")
        warm = keep.tile([P, 1], F32, name="warm", tag="warm", align_bytes=64)
        nc.vector.memset(scales[:].bitcast(I32), 0)
        nc.vector.memset(one[:], 1.0)
        nc.scalar.activation(out=warm[:], in_=one[:], func=ACT.Abs_reciprocal_sqrt)

        words = {}

        def load_words(o):
            words[o] = keep.tile([P, T], U32, name="words%d" % o, tag=("words0", "w_raw")[o], align_bytes=64)
            nc.sync.dma_start(out=words[o][:].bitcast(I32), in_=x_words[o].rearrange("p c r -> p (c r)").bitcast(I32))

        w_raw = keep.tile([P, PASSES, PACK, N], F32, name="w_raw", tag="w_raw", align_bytes=64)
        grouped = keep.tile([P, PASSES, N, PACK], BF16, name="grouped", align_bytes=64)
        w_codes = keep.tile([P, PASSES, N], U32, name="w_codes", align_bytes=64)
        w_scales = keep.tile([P, PASSES, N], U8, name="w_scales", align_bytes=64)

        nc.sync.dma_start(offs_sb[:], offs)
        nc.sync.dma_start(out=w_raw[:], in_=w1.rearrange("(o p j) m -> p o j m", o=PASSES, j=PACK))
        load_words(0)
        nc.sync.dma_start(nbr_sb[:], nbr)
        nc.sync.dma_start(out=rest_sb[:], in_=rest)
        for q in range(2):
            nc.gpsimd.dma_start(
                out=scales[32 * q : 32 * q + 4 * PASSES, :].bitcast(I32),
                in_=x_scales[:, 4 * q : 4 * q + 4, :].bitcast(I32),
            )
        for q in range(2, 4):
            for o in range(PASSES):
                nc.sync.dma_start(
                    out=scales[32 * q + 4 * o : 32 * q + 4 * o + 4, :].bitcast(I32),
                    in_=x_scales[o, 4 * q : 4 * q + 4, :].bitcast(I32),
                )
        nc.scalar.copy(out=grouped[:], in_=w_raw[:].rearrange("p o j m -> p o m j"))
        load_words(1)
        nc.scalar.activation(out=rest_scaled[:], in_=rest_sb[:], func=ACT.Copy, scale=-0.2)

        picked_scales = keep.tile([P, S], U8, name="picked_scales", align_bytes=64)
        y = [psum.tile([N, width], F32, name="y%d" % c) for c, width in enumerate(CHUNKS)]

        def pick_words(o):
            picked = []
            for h in range(2):
                tag = (("picked_a", "picked_b"), ("scales", "picked_a"))[o][h]
                half = keep.tile([P, HALF], U32, name="picked%d_%d" % (o, h), tag=tag, align_bytes=64)
                cols = slice(h * HALF // LIST_ROWS, (h + 1) * HALF // LIST_ROWS)
                nc.vector.tensor_copy(half[:], words[o][:].indirect(offs_sb[:, cols]))
                picked.append(half)
            return picked

        def multiply(o, picked):
            for c in range(len(CHUNKS)):
                cols = slice(STARTS[c], STARTS[c + 1])
                nc.tensor.matmul_mx(
                    out=y[c][:],
                    lhsT=w_codes[:, o, :].bitcast(FP8X4),
                    lhsT_scale=w_scales[:, o, :],
                    rhs=picked[STARTS[c] // HALF][:, STARTS[c] % HALF : STARTS[c] % HALF + CHUNKS[c]].bitcast(FP8X4),
                    rhs_scale=picked_scales[4 * o : P, cols],
                    start=(o == 0),
                    stop=(o == PASSES - 1),
                )

        nc.vector.tensor_copy(picked_scales[:], scales[:].indirect(offs_sb[:]))
        picked0 = pick_words(0)
        nc.vector.quantize_mx(
            out=w_codes[:].rearrange("p o m -> p (o m)").bitcast(FP8X4),
            scales=w_scales[:].rearrange("p o m -> p (o m)"),
            in_=grouped[:].rearrange("p o m j -> p (o m j)"),
        )
        multiply(0, picked0)
        multiply(1, pick_words(1))

        ysq = [keep.tile([N, width], F32, name="ysq%d" % c) for c, width in enumerate(CHUNKS)]
        u = [keep.tile([N, width], F32, name="u%d" % c) for c, width in enumerate(CHUNKS)]
        uy = keep.tile([N, S], F32, name="uy")
        ker = [uy[:, STARTS[c] : STARTS[c + 1]] for c in range(len(CHUNKS))]
        ksum = keep.tile([N, V], F32, name="ksum")
        table = keep.tile([N, 3 * V], F32, name="table")
        q_all, inv, dsq = table[:, 0:V], table[:, V : 2 * V], table[:, 2 * V : 3 * V]

        def square(c):
            nc.scalar.activation(out=ysq[c][:], in_=y[c][:], func=ACT.Square)

        def clamp(c):
            if CLAMP_ENGINE[c] == "S":
                nc.scalar.activation(out=u[c][:], in_=ysq[c][:], func=ACT.Relu, scale=-1.0, bias=5.0)
            elif CLAMP_ENGINE[c] == "V":
                nc.vector.tensor_scalar(
                    out=u[c][:], in0=ysq[c][:], scalar1=5.0, scalar2=5.0, op0=ALU.min, op1=ALU.subtract
                )
            else:
                nc.gpsimd.tensor_scalar(
                    out=u[c][:], in0=ysq[c][:], scalar1=5.0, scalar2=0.0, op0=ALU.min, op1=ALU.max
                )

        def kernel_value(c):
            if KER_ENGINE[c] == "V":
                nc.vector.scalar_tensor_tensor(
                    out=ker[c], in0=u[c][:], scalar=0.04, in1=u[c][:], op0=ALU.mult, op1=ALU.mult
                )
            elif CLAMP_ENGINE[c] == "G":
                nc.scalar.activation(out=ker[c], in_=u[c][:], func=ACT.Square, scale=-0.2, bias=1.0)
            else:
                nc.scalar.activation(out=ker[c], in_=u[c][:], func=ACT.Square, scale=0.2)

        def density(c):
            groups = slice(STARTS[c] // D, STARTS[c + 1] // D)
            nc.vector.tensor_reduce(
                out=ksum[:, groups], in_=ker[c].rearrange("m (v d) -> m v d", d=D), axis=AX.X, op=ALU.add
            )

        def pressure(g):
            first, last = PRESSURE_CUTS[g], PRESSURE_CUTS[g + 1]
            groups = slice(STARTS[first] // D, STARTS[last] // D)
            nc.scalar.activation(out=dsq[:, groups], in_=ksum[:, groups], func=ACT.Square, bias=0.6)
            nc.scalar.activation(out=inv[:, groups], in_=dsq[:, groups], func=ACT.Abs_reciprocal_sqrt)
            nc.vector.scalar_tensor_tensor(
                out=q_all[:, groups],
                in0=inv[:, groups],
                scalar=rest_scaled[:],
                in1=inv[:, groups],
                op0=ALU.mult,
                op1=ALU.mult,
            )

        def slope(c):
            cols = slice(STARTS[c], STARTS[c + 1])
            scalar, op0 = {"S": (-1.0, ALU.mult), "V": (1.0, ALU.mult), "G": (5.0, ALU.subtract)}[CLAMP_ENGINE[c]]
            nc.vector.scalar_tensor_tensor(
                out=uy[:, cols], in0=u[c][:], scalar=scalar, in1=y[c][:], op0=op0, op1=ALU.mult
            )

        steps = {"s": square, "m": clamp, "k": kernel_value, "r": density, "p": pressure, "y": slope}
        for step in ORDER:
            steps[step[0]](int(step[1]))

        first = 0
        for i, width in enumerate(FAR):
            last = first + width
            cols = slice(first, last)
            count = width // D
            own = keep.tile([N, width], F32, name="own%d" % i)
            both = keep.tile([N, width], F32, name="both%d" % i)
            force = keep.tile([N, width], F32, name="force%d" % i)
            nc.scalar.activation(
                out=own[:].rearrange("m (v d) -> m v d", d=D),
                in_=q_all[:, first // D : last // D].unsqueeze(2).to_broadcast([N, count, D]),
                func=ACT.Identity,
                bias=-0.4,
            )
            nc.vector.tensor_tensor(
                both[:],
                table[:].indirect(nbr_sb[:, first // LIST_ROWS : last // LIST_ROWS]),
                own[:],
                ALU.add,
            )
            nc.vector.tensor_tensor(out=force[:], in0=both[:], in1=uy[:, cols], op=ALU.mult)
            nc.sync.dma_start(out=out[:, cols], in_=force[:])
            first = last
